import numpy as np
import ml_dtypes


def mxq(x, axis, fmt="e4m3"):
    dtype, down = {"e4m3": (ml_dtypes.float8_e4m3fn, 7), "e5m2": (ml_dtypes.float8_e5m2, 14)}[fmt]
    v = np.moveaxis(np.asarray(x, np.float32).astype(ml_dtypes.bfloat16).astype(np.float64), axis, -1)
    blocks = v.reshape(v.shape[:-1] + (-1, 32))
    amax = np.abs(blocks).max(-1, keepdims=True)
    byte = np.maximum(np.where(amax > 0, np.frexp(amax)[1] - 1 + 127, 0) - down, 1)
    scale = np.exp2(byte - 127.0)
    codes = (blocks / scale).astype(np.float32).astype(dtype).astype(np.float64)
    return np.moveaxis((codes * scale).reshape(v.shape), -1, axis)


WIDE = False


def mx_kscale(k):
    if not WIDE:
        return np.ones(k)
    levels = np.array([10, -10, 5, -5, 0])
    if k % 512:
        return np.exp2(np.random.permutation(np.resize(levels, k // 32))).repeat(32)
    a = np.empty((k // 512, 16))
    for p in range(k // 512):
        a[p, :8] = np.random.permutation(np.resize(levels, 8))
        for g in range(8):
            far = levels[np.abs(levels - a[p, g]) >= 10]
            a[p, g + 8] = far[np.random.randint(len(far))]
    return np.exp2(a.ravel()).repeat(32)


def f64(x):
    return np.asarray(x).astype(np.float64)


def striped(idx):
    return np.tile(idx.reshape(-1, 16).T, (8, 1)).astype(np.uint16)


def unstriped(offs):
    return offs[:16].T.reshape(-1).astype(np.int64)


def striped8(idx):
    return np.concatenate([x.reshape(-1, 16).T for x in idx]).astype(np.uint16)


def runs(offs, k):
    lists = np.stack([offs[16 * r : 16 * r + 16].T.reshape(-1) for r in range(8)]).astype(np.int64)
    return lists[np.arange(k) % 512 // 64]


def pack_weight(w):
    k, n = w.shape
    w = f64(np.asarray(w, np.float32).astype(ml_dtypes.bfloat16)).reshape(k // 32, 32, n)
    amax = np.abs(w).max(1)
    byte = np.clip(np.where(amax > 0, np.frexp(amax)[1] - 1 + 127 - 7, 1), 1, 254)
    scaled = (w * np.exp2(127.0 - byte)[:, None, :]).reshape(k, n).astype(np.float32)
    words = np.ascontiguousarray(scaled.reshape(k // 512, 128, 4, n).transpose(0, 1, 3, 2)).astype(ml_dtypes.float8_e4m3fn).view(np.uint8)
    return words, np.ascontiguousarray(byte.astype(np.uint8).reshape(k // 512, 16, n))


def unpack_weight(words, scales):
    g, p, n, _ = words.shape
    vals = np.ascontiguousarray(words).view(ml_dtypes.float8_e4m3fn).astype(np.float64) * np.repeat(np.exp2(scales.astype(np.float64) - 127.0), 8, axis=1)[..., None]
    return vals.transpose(0, 1, 3, 2).reshape(g * 512, n)


K, T, S, V, N = 1024, 2048, 512, 512, 512


def setup_inputs():
    n = np.random.standard_normal
    s = mx_kscale(K)[:, None]
    packed_xT = pack_weight(n((K, T)) * s)
    return {
        "x_words": packed_xT[0],
        "x_scales": packed_xT[1],
        "w1": (n((K, N)) / np.sqrt(K) / s).astype(np.float32),
        "w2": (n((K, N)) / np.sqrt(K) / s).astype(np.float32),
        "offs": striped(np.random.permutation(T)[:S]),
        "coarse": striped(np.random.permutation(T)[:V]),
        "par": striped8(np.random.randint(0, V, (8, S))),
    }


def reference(x_words, x_scales, w1, w2, offs, coarse, par):
    xq = unpack_weight(x_words, x_scales)[:, unstriped(offs)]
    y = mxq(f64(w1), 0, "e4m3").T @ xq
    e = np.exp(y - y.max(axis=1, keepdims=True))
    fs = e / e.sum(axis=1, keepdims=True)
    x_coarse = unpack_weight(x_words, x_scales)[:, unstriped(coarse)]
    c = mxq(f64(w2), 0, "e4m3").T @ x_coarse
    e = np.exp(c - c.max(axis=1, keepdims=True))
    cs = e / e.sum(axis=1, keepdims=True)
    return 512.0 * (fs * (cs[np.arange(N)[:, None], runs(par, N)]))

@@ -1,0 +1,176 @@
+from contextlib import ExitStack
+
+import concourse.mybir as mybir
+
+K, T, S, N = 1024, 2048, 512, 512
+FLOPS = 2 * 2 * K * N * S
+
+F32 = mybir.dt.float32
+BF16 = mybir.dt.bfloat16
+I32 = mybir.dt.int32
+U32 = mybir.dt.uint32
+U16 = mybir.dt.uint16
+U8 = mybir.dt.uint8
+FP8X4 = mybir.dt.float8_e4m3fn_x4
+ALU = mybir.AluOpType
+ACT = mybir.ActivationFunctionType
+AXIS_X = mybir.AxisListType.X
+
+P = 128
+PACK = 4
+PASSES = K // (P * PACK)
+TILES = N // P
+HALF = S // 2
+
+
+def tile_picked_hiersm_none_p_kernel(
+    tc, x_words, x_scales, w1, w2, offs, coarse, par, out
+):
+    nc = tc.nc
+    with ExitStack() as ctx:
+        lists = ctx.enter_context(tc.tile_pool(name="lists", bufs=1))
+        keep = ctx.enter_context(tc.tile_pool(name="keep", bufs=1))
+        psum = ctx.enter_context(tc.psum_pool(name="psum", bufs=1))
+
+        table_scales = keep.tile([P, T], U8, name="table_scales", align_bytes=64)
+        nc.vector.memset(table_scales[:].bitcast(I32), 0)
+
+        warm = keep.tile([P, 2], F32, name="warm")
+        nc.vector.memset(warm[:, 0:1], 0.0)
+        nc.scalar.activation(warm[:, 1:2], warm[:, 0:1], ACT.Exp)
+
+        def load_words(z):
+            words = keep.tile([P, T], I32, name="table_words%d" % z, align_bytes=64)
+            nc.sync.dma_start(words[:], x_words[z].rearrange("p n r -> p (n r)").bitcast(I32))
+            return words
+
+        def load_list(src, name):
+            tile = lists.tile([P, S // 16], U16, name=name)
+            nc.sync.dma_start(tile[:], src)
+            return tile
+
+        def load_weight(w, z, name):
+            raw = keep.tile([P, PACK, N], F32, name="%s_raw%d" % (name, z), align_bytes=64)
+            nc.sync.dma_start(raw[:], w[512 * z : 512 * (z + 1), :].rearrange("(p j) c -> p j c", j=PACK))
+            return raw
+
+        words0 = load_words(0)
+        coarse_list = load_list(coarse, "coarse_list")
+        offs_list = load_list(offs, "offs_list")
+        for q in range(4):
+            nc.sync.dma_start(
+                table_scales[32 * q : 32 * q + 4 * PASSES, :].bitcast(I32),
+                x_scales[:, 4 * q : 4 * q + 4, :].bitcast(I32),
+            )
+        w2_raw0 = load_weight(w2, 0, "w2")
+        words1 = load_words(1)
+        w2_raw1 = load_weight(w2, 1, "w2")
+        w1_raw0 = load_weight(w1, 0, "w1")
+        w1_raw1 = load_weight(w1, 1, "w1")
+        par_list = load_list(par, "par_list")
+
+        def gather_words(words, index, name):
+            picked = keep.tile([P, S], U32, name=name, align_bytes=64)
+            nc.vector.tensor_copy(picked[:], words[:].bitcast(U32).indirect(index[:]))
+            return picked
+
+        def gather_scales(index, name):
+            picked = keep.tile([P, S], U8, name=name, align_bytes=64)
+            nc.vector.tensor_copy(picked[:], table_scales[:].indirect(index[:]))
+            return picked
+
+        def cast(raw, t, name):
+            grouped = keep.tile([P, P * PACK], BF16, name="%s_bf%d" % (name, t), align_bytes=64)
+            nc.scalar.copy(
+                grouped[:].rearrange("p (a b j) -> p a j b", b=4, j=PACK),
+                raw[:].rearrange("p j (a t b) -> p t a j b", t=TILES, b=4)[:, t],
+            )
+            return grouped
+
+        def quantize(grouped, t, name):
+            codes = keep.tile([P, P], U32, name="%s_codes%d" % (name, t), align_bytes=64)
+            scales = keep.tile([P, P], U8, name="%s_scales%d" % (name, t), align_bytes=64)
+            nc.vector.quantize_mx(out=codes[:].bitcast(FP8X4), scales=scales[:], in_=grouped[:])
+            return codes, scales
+
+        def multiply(bank, weights, picked_words, picked_scales, z):
+            codes, scales = weights
+            nc.tensor.matmul_mx(
+                out=bank[:],
+                lhsT=codes[:].bitcast(FP8X4),
+                lhsT_scale=scales[:],
+                rhs=picked_words[:].bitcast(FP8X4),
+                rhs_scale=picked_scales[4 * z : P, :],
+                start=(z == 0),
+                stop=(z == PASSES - 1),
+            )
+
+        c_banks = [psum.tile([P, S], F32, name="c_bank%d" % t) for t in range(TILES)]
+        y_banks = [psum.tile([P, S], F32, name="y_bank%d" % t) for t in range(TILES)]
+
+        coarse_words0 = gather_words(words0, coarse_list, "coarse_words0")
+        fine_words0 = gather_words(words0, offs_list, "fine_words0")
+        coarse_scales = gather_scales(coarse_list, "coarse_scales")
+        fine_scales = gather_scales(offs_list, "fine_scales")
+        w2_bf0 = [cast(w2_raw0, t, "w2p0") for t in range(TILES)]
+        coarse_words1 = gather_words(words1, coarse_list, "coarse_words1")
+        for t in range(TILES):
+            multiply(c_banks[t], quantize(w2_bf0[t], t, "w2p0"), coarse_words0, coarse_scales, 0)
+        fine_words1 = gather_words(words1, offs_list, "fine_words1")
+
+        def neg_max(bank, name):
+            top = keep.tile([P, 1], F32, name=name)
+            nc.vector.tensor_reduce(top[:], bank[:], AXIS_X, ALU.max, negate=True)
+            return top
+
+        def exp_rows(bank, top, name):
+            vals = keep.tile([P, S], F32, name=name, align_bytes=64)
+            total = keep.tile([P, 1], F32, name=name + "_sum")
+            nc.scalar.activation(vals[:], bank[:], ACT.Exp, bias=top[:], accum_out=total[:])
+            return vals, total
+
+        c_top = []
+        for t in range(TILES):
+            multiply(c_banks[t], quantize(cast(w2_raw1, t, "w2p1"), t, "w2p1"), coarse_words1, coarse_scales, 1)
+            if t > 0:
+                c_top.append(neg_max(c_banks[t - 1], "c_top%d" % (t - 1)))
+        c_top.append(neg_max(c_banks[TILES - 1], "c_top%d" % (TILES - 1)))
+        for t in range(TILES):
+            multiply(y_banks[t], quantize(cast(w1_raw0, t, "w1p0"), t, "w1p0"), fine_words0, fine_scales, 0)
+        y_top = []
+        for t in range(TILES):
+            multiply(y_banks[t], quantize(cast(w1_raw1, t, "w1p1"), t, "w1p1"), fine_words1, fine_scales, 1)
+            if t > 0:
+                y_top.append(neg_max(y_banks[t - 1], "y_top%d" % (t - 1)))
+        y_top.append(neg_max(y_banks[TILES - 1], "y_top%d" % (TILES - 1)))
+
+        out_rows = out.rearrange("(a t b) j -> t a b j", t=TILES, b=4)
+        pending = []
+
+        def finish(item):
+            prod, factor, t = item
+            res = keep.tile([P, S], F32, name="res%d" % t, align_bytes=64)
+            nc.scalar.activation(res[:], prod[:], ACT.Copy, scale=factor[:])
+            nc.sync.dma_start(out_rows[t], res[:])
+
+        for t in range(TILES):
+            c_exp, c_sum = exp_rows(c_banks[t], c_top[t], "c_exp%d" % t)
+            y_exp, y_sum = exp_rows(y_banks[t], y_top[t], "y_exp%d" % t)
+            both = keep.tile([P, 1], F32, name="both%d" % t)
+            factor = keep.tile([P, 1], F32, name="factor%d" % t)
+            prod = keep.tile([P, S], F32, name="prod%d" % t, align_bytes=64)
+            nc.vector.tensor_scalar(both[:], y_sum[:], c_sum[:], 1.0 / 512.0, ALU.mult, ALU.mult)
+            for h in range(2):
+                cols = slice(h * HALF, (h + 1) * HALF)
+                nc.vector.tensor_tensor(
+                    prod[:, cols],
+                    c_exp[:].indirect(par_list[:, h * HALF // 16 : (h + 1) * HALF // 16]),
+                    y_exp[:, cols],
+                    ALU.mult,
+                )
+                if h == 0:
+                    nc.vector.reciprocal(factor[:], both[:])
+            if pending:
+                finish(pending.pop())
+            pending.append((prod, factor, t))
+        finish(pending.pop())

@@ -21,6 +21,7 @@ PACK = 4
 PASSES = K // (P * PACK)
 TILES = N // P
 HALF = S // 2
+ENG = {("w1p1", 2): "vector", ("w1p1", 3): "vector"}
 
 
 def tile_picked_hiersm_none_p_kernel(
@@ -39,6 +40,10 @@ def tile_picked_hiersm_none_p_kernel(
         nc.vector.memset(warm[:, 0:1], 0.0)
         nc.scalar.activation(warm[:, 1:2], warm[:, 0:1], ACT.Exp)
 
+        windows = [keep.tile([P, 2 * S], F32, name="window%d" % t, align_bytes=64) for t in range(TILES)]
+        for t in range(TILES):
+            nc.vector.memset(windows[t][:, S:], 0.0)
+
         def load_words(z):
             words = keep.tile([P, T], I32, name="table_words%d" % z, align_bytes=64)
             nc.sync.dma_start(words[:], x_words[z].rearrange("p n r -> p (n r)").bitcast(I32))
@@ -49,6 +54,13 @@ def tile_picked_hiersm_none_p_kernel(
             nc.sync.dma_start(tile[:], src)
             return tile
 
+        def load_scales():
+            for q in range(4):
+                nc.sync.dma_start(
+                    table_scales[32 * q : 32 * q + 4 * PASSES, :].bitcast(I32),
+                    x_scales[:, 4 * q : 4 * q + 4, :].bitcast(I32),
+                )
+
         def load_weight(w, z, name):
             raw = keep.tile([P, PACK, N], F32, name="%s_raw%d" % (name, z), align_bytes=64)
             nc.sync.dma_start(raw[:], w[512 * z : 512 * (z + 1), :].rearrange("(p j) c -> p j c", j=PACK))
@@ -57,11 +69,7 @@ def tile_picked_hiersm_none_p_kernel(
         words0 = load_words(0)
         coarse_list = load_list(coarse, "coarse_list")
         offs_list = load_list(offs, "offs_list")
-        for q in range(4):
-            nc.sync.dma_start(
-                table_scales[32 * q : 32 * q + 4 * PASSES, :].bitcast(I32),
-                x_scales[:, 4 * q : 4 * q + 4, :].bitcast(I32),
-            )
+        load_scales()
         w2_raw0 = load_weight(w2, 0, "w2")
         words1 = load_words(1)
         w2_raw1 = load_weight(w2, 1, "w2")
@@ -79,31 +87,54 @@ def tile_picked_hiersm_none_p_kernel(
             nc.vector.tensor_copy(picked[:], table_scales[:].indirect(index[:]))
             return picked
 
-        def cast(raw, t, name):
-            grouped = keep.tile([P, P * PACK], BF16, name="%s_bf%d" % (name, t), align_bytes=64)
-            nc.scalar.copy(
-                grouped[:].rearrange("p (a b j) -> p a j b", b=4, j=PACK),
-                raw[:].rearrange("p j (a t b) -> p t a j b", t=TILES, b=4)[:, t],
-            )
-            return grouped
+        def cast(grouped, raw, t, engine="scalar"):
+            dst = grouped.rearrange("p (a b j) -> p a j b", b=4, j=PACK)
+            src = raw[:].rearrange("p j (a t b) -> p t a j b", t=TILES, b=4)[:, t]
+            if engine == "vector":
+                nc.vector.tensor_copy(dst, src)
+            elif engine == "gpsimd":
+                nc.gpsimd.tensor_scalar(dst, src, 1.0, 0.0, ALU.mult, ALU.add)
+            else:
+                nc.scalar.copy(dst, src)
 
-        def quantize(grouped, t, name):
-            codes = keep.tile([P, P], U32, name="%s_codes%d" % (name, t), align_bytes=64)
-            scales = keep.tile([P, P], U8, name="%s_scales%d" % (name, t), align_bytes=64)
+        def quantize(grouped, name):
+            width = grouped.shape[1] // PACK
+            codes = keep.tile([P, width], U32, name=name + "_codes", align_bytes=64)
+            scales = keep.tile([P, width], U8, name=name + "_scales", align_bytes=64)
             nc.vector.quantize_mx(out=codes[:].bitcast(FP8X4), scales=scales[:], in_=grouped[:])
             return codes, scales
 
-        def multiply(bank, weights, picked_words, picked_scales, z):
-            codes, scales = weights
+        def multiply(bank, codes, scales, picked_words, picked_scales, z):
             nc.tensor.matmul_mx(
                 out=bank[:],
-                lhsT=codes[:].bitcast(FP8X4),
-                lhsT_scale=scales[:],
+                lhsT=codes.bitcast(FP8X4),
+                lhsT_scale=scales,
                 rhs=picked_words[:].bitcast(FP8X4),
                 rhs_scale=picked_scales[4 * z : P, :],
                 start=(z == 0),
                 stop=(z == PASSES - 1),
             )
+
+        def first_pass(banks, raw, picked_words, picked_scales, name):
+            for t0 in range(0, TILES, 1):
+                grouped = keep.tile([P, 1 * P * PACK], BF16, name="%s_bf%d" % (name, t0), align_bytes=64)
+                for u in range(1):
+                    cast(grouped[:, u * P * PACK : (u + 1) * P * PACK], raw, t0 + u, ENG.get((name, t0 + u), "scalar"))
+                codes, scales = quantize(grouped, "%s_%d" % (name, t0))
+                for u in range(1):
+                    cols = slice(u * P, (u + 1) * P)
+                    multiply(banks[t0 + u], codes[:, cols], scales[:, cols], picked_words, picked_scales, 0)
+
+        def last_pass(bank, raw, t, picked_words, picked_scales, name):
+            grouped = keep.tile([P, P * PACK], BF16, name="%s_bf%d" % (name, t), align_bytes=64)
+            cast(grouped[:], raw, t, ENG.get((name, t), "scalar"))
+            codes, scales = quantize(grouped, "%s_%d" % (name, t))
+            multiply(bank, codes[:], scales[:], picked_words, picked_scales, 1)
+
+        def neg_max(bank, name):
+            top = keep.tile([P, 1], F32, name=name)
+            nc.vector.tensor_reduce(top[:], bank[:], AXIS_X, ALU.max, negate=True)
+            return top
 
         c_banks = [psum.tile([P, S], F32, name="c_bank%d" % t) for t in range(TILES)]
         y_banks = [psum.tile([P, S], F32, name="y_bank%d" % t) for t in range(TILES)]
@@ -112,65 +143,59 @@ def tile_picked_hiersm_none_p_kernel(
         fine_words0 = gather_words(words0, offs_list, "fine_words0")
         coarse_scales = gather_scales(coarse_list, "coarse_scales")
         fine_scales = gather_scales(offs_list, "fine_scales")
-        w2_bf0 = [cast(w2_raw0, t, "w2p0") for t in range(TILES)]
+        first_pass(c_banks, w2_raw0, coarse_words0, coarse_scales, "w2p0")
         coarse_words1 = gather_words(words1, coarse_list, "coarse_words1")
-        for t in range(TILES):
-            multiply(c_banks[t], quantize(w2_bf0[t], t, "w2p0"), coarse_words0, coarse_scales, 0)
         fine_words1 = gather_words(words1, offs_list, "fine_words1")
 
-        def neg_max(bank, name):
-            top = keep.tile([P, 1], F32, name=name)
-            nc.vector.tensor_reduce(top[:], bank[:], AXIS_X, ALU.max, negate=True)
-            return top
-
-        def exp_rows(bank, top, name):
-            vals = keep.tile([P, S], F32, name=name, align_bytes=64)
-            total = keep.tile([P, 1], F32, name=name + "_sum")
-            nc.scalar.activation(vals[:], bank[:], ACT.Exp, bias=top[:], accum_out=total[:])
-            return vals, total
-
-        c_top = []
         for t in range(TILES):
-            multiply(c_banks[t], quantize(cast(w2_raw1, t, "w2p1"), t, "w2p1"), coarse_words1, coarse_scales, 1)
-            if t > 0:
-                c_top.append(neg_max(c_banks[t - 1], "c_top%d" % (t - 1)))
-        c_top.append(neg_max(c_banks[TILES - 1], "c_top%d" % (TILES - 1)))
+            last_pass(c_banks[t], w2_raw1, t, coarse_words1, coarse_scales, "w2p1")
+        c_top = [neg_max(c_banks[t], "c_top%d" % t) for t in range(TILES)]
+        c_sum = keep.tile([P, TILES], F32, name="c_sum")
+        y_sum = keep.tile([P, TILES], F32, name="y_sum")
+        first_pass(y_banks, w1_raw0, fine_words0, fine_scales, "w1p0")
         for t in range(TILES):
-            multiply(y_banks[t], quantize(cast(w1_raw0, t, "w1p0"), t, "w1p0"), fine_words0, fine_scales, 0)
-        y_top = []
-        for t in range(TILES):
-            multiply(y_banks[t], quantize(cast(w1_raw1, t, "w1p1"), t, "w1p1"), fine_words1, fine_scales, 1)
-            if t > 0:
-                y_top.append(neg_max(y_banks[t - 1], "y_top%d" % (t - 1)))
-        y_top.append(neg_max(y_banks[TILES - 1], "y_top%d" % (TILES - 1)))
+            last_pass(y_banks[t], w1_raw1, t, fine_words1, fine_scales, "w1p1")
+        y_top = [neg_max(y_banks[t], "y_top%d" % t) for t in range(TILES)]
 
         out_rows = out.rearrange("(a t b) j -> t a b j", t=TILES, b=4)
-        pending = []
+        both = keep.tile([P, TILES], F32, name="both")
+        factor = keep.tile([P, TILES], F32, name="factor")
+        y_exp = [keep.tile([P, S], F32, name="y_exp%d" % t, align_bytes=64) for t in range(TILES)]
+        prod = [keep.tile([P, S], F32, name="prod%d" % t, align_bytes=64) for t in range(TILES)]
+        scaled = [keep.tile([P, S], F32, name="scaled%d" % t, align_bytes=64) for t in range(TILES)]
 
-        def finish(item):
-            prod, factor, t = item
-            res = keep.tile([P, S], F32, name="res%d" % t, align_bytes=64)
-            nc.scalar.activation(res[:], prod[:], ACT.Copy, scale=factor[:])
-            nc.sync.dma_start(out_rows[t], res[:])
+        def exps(t):
+            nc.scalar.activation(windows[t][:, :S], c_banks[t][:], ACT.Exp, bias=c_top[t][:], accum_out=c_sum[:, t : t + 1])
+            nc.scalar.activation(y_exp[t][:], y_banks[t][:], ACT.Exp, bias=y_top[t][:], accum_out=y_sum[:, t : t + 1])
 
-        for t in range(TILES):
-            c_exp, c_sum = exp_rows(c_banks[t], c_top[t], "c_exp%d" % t)
-            y_exp, y_sum = exp_rows(y_banks[t], y_top[t], "y_exp%d" % t)
-            both = keep.tile([P, 1], F32, name="both%d" % t)
-            factor = keep.tile([P, 1], F32, name="factor%d" % t)
-            prod = keep.tile([P, S], F32, name="prod%d" % t, align_bytes=64)
-            nc.vector.tensor_scalar(both[:], y_sum[:], c_sum[:], 1.0 / 512.0, ALU.mult, ALU.mult)
-            for h in range(2):
-                cols = slice(h * HALF, (h + 1) * HALF)
-                nc.vector.tensor_tensor(
-                    prod[:, cols],
-                    c_exp[:].indirect(par_list[:, h * HALF // 16 : (h + 1) * HALF // 16]),
-                    y_exp[:, cols],
-                    ALU.mult,
-                )
-                if h == 0:
-                    nc.vector.reciprocal(factor[:], both[:])
-            if pending:
-                finish(pending.pop())
-            pending.append((prod, factor, t))
-        finish(pending.pop())
+        def sums(cols):
+            nc.vector.scalar_tensor_tensor(both[:, cols], y_sum[:, cols], 1.0 / 512.0, c_sum[:, cols], ALU.mult, ALU.mult)
+
+        def times_parent(t, fine):
+            nc.vector.tensor_tensor(prod[t][:], windows[t][:].indirect(par_list[:]), fine[:], ALU.mult)
+
+        def scale(t, vals):
+            nc.scalar.activation(scaled[t][:], vals[:], ACT.Copy, scale=factor[:, t : t + 1])
+
+        exps(0)
+        times_parent(0, y_exp[0])
+        exps(1)
+        sums(slice(0, 2))
+        nc.vector.reciprocal(factor[:, 0:2], both[:, 0:2])
+        times_parent(1, y_exp[1])
+        exps(2)
+        sums(slice(2, 3))
+        nc.vector.reciprocal(factor[:, 2:3], both[:, 2:3])
+        exps(3)
+        sums(slice(3, 4))
+        times_parent(3, y_exp[3])
+        nc.vector.reciprocal(factor[:, 3:4], both[:, 3:4])
+        scale(0, prod[0])
+        nc.sync.dma_start(out_rows[0], scaled[0][:])
+        scale(2, y_exp[2])
+        times_parent(2, scaled[2])
+        scale(1, prod[1])
+        nc.sync.dma_start(out_rows[1], scaled[1][:])
+        scale(3, prod[3])
+        nc.scalar.dma_start(out_rows[3], scaled[3][:])
+        nc.sync.dma_start(out_rows[2], prod[2][:])

from contextlib import ExitStack

import concourse.mybir as mybir

K, T, S, N = 1024, 2048, 512, 512
FLOPS = 2 * 2 * K * N * S

F32 = mybir.dt.float32
BF16 = mybir.dt.bfloat16
I32 = mybir.dt.int32
U32 = mybir.dt.uint32
U16 = mybir.dt.uint16
U8 = mybir.dt.uint8
FP8X4 = mybir.dt.float8_e4m3fn_x4
ALU = mybir.AluOpType
ACT = mybir.ActivationFunctionType
AXIS_X = mybir.AxisListType.X

P = 128
PACK = 4
PASSES = K // (P * PACK)
TILES = N // P
HALF = S // 2
ENG = {("w1p1", 2): "vector", ("w1p1", 3): "vector"}


def tile_picked_hiersm_none_p_kernel(
    tc, x_words, x_scales, w1, w2, offs, coarse, par, out
):
    nc = tc.nc
    with ExitStack() as ctx:
        lists = ctx.enter_context(tc.tile_pool(name="lists", bufs=1))
        keep = ctx.enter_context(tc.tile_pool(name="keep", bufs=1))
        psum = ctx.enter_context(tc.psum_pool(name="psum", bufs=1))

        table_scales = keep.tile([P, T], U8, name="table_scales", align_bytes=64)
        nc.vector.memset(table_scales[:].bitcast(I32), 0)

        warm = keep.tile([P, 2], F32, name="warm")
        nc.vector.memset(warm[:, 0:1], 0.0)
        nc.scalar.activation(warm[:, 1:2], warm[:, 0:1], ACT.Exp)

        windows = [keep.tile([P, 2 * S], F32, name="window%d" % t, align_bytes=64) for t in range(TILES)]
        for t in range(TILES):
            nc.vector.memset(windows[t][:, S:], 0.0)

        def load_words(z):
            words = keep.tile([P, T], I32, name="table_words%d" % z, align_bytes=64)
            nc.sync.dma_start(words[:], x_words[z].rearrange("p n r -> p (n r)").bitcast(I32))
            return words

        def load_list(src, name):
            tile = lists.tile([P, S // 16], U16, name=name)
            nc.sync.dma_start(tile[:], src)
            return tile

        def load_scales():
            for q in range(4):
                nc.sync.dma_start(
                    table_scales[32 * q : 32 * q + 4 * PASSES, :].bitcast(I32),
                    x_scales[:, 4 * q : 4 * q + 4, :].bitcast(I32),
                )

        def load_weight(w, z, name):
            raw = keep.tile([P, PACK, N], F32, name="%s_raw%d" % (name, z), align_bytes=64)
            nc.sync.dma_start(raw[:], w[512 * z : 512 * (z + 1), :].rearrange("(p j) c -> p j c", j=PACK))
            return raw

        words0 = load_words(0)
        coarse_list = load_list(coarse, "coarse_list")
        offs_list = load_list(offs, "offs_list")
        load_scales()
        w2_raw0 = load_weight(w2, 0, "w2")
        words1 = load_words(1)
        w2_raw1 = load_weight(w2, 1, "w2")
        w1_raw0 = load_weight(w1, 0, "w1")
        w1_raw1 = load_weight(w1, 1, "w1")
        par_list = load_list(par, "par_list")

        def gather_words(words, index, name):
            picked = keep.tile([P, S], U32, name=name, align_bytes=64)
            nc.vector.tensor_copy(picked[:], words[:].bitcast(U32).indirect(index[:]))
            return picked

        def gather_scales(index, name):
            picked = keep.tile([P, S], U8, name=name, align_bytes=64)
            nc.vector.tensor_copy(picked[:], table_scales[:].indirect(index[:]))
            return picked

        def cast(grouped, raw, t, engine="scalar"):
            dst = grouped.rearrange("p (a b j) -> p a j b", b=4, j=PACK)
            src = raw[:].rearrange("p j (a t b) -> p t a j b", t=TILES, b=4)[:, t]
            if engine == "vector":
                nc.vector.tensor_copy(dst, src)
            elif engine == "gpsimd":
                nc.gpsimd.tensor_scalar(dst, src, 1.0, 0.0, ALU.mult, ALU.add)
            else:
                nc.scalar.copy(dst, src)

        def quantize(grouped, name):
            width = grouped.shape[1] // PACK
            codes = keep.tile([P, width], U32, name=name + "_codes", align_bytes=64)
            scales = keep.tile([P, width], U8, name=name + "_scales", align_bytes=64)
            nc.vector.quantize_mx(out=codes[:].bitcast(FP8X4), scales=scales[:], in_=grouped[:])
            return codes, scales

        def multiply(bank, codes, scales, picked_words, picked_scales, z):
            nc.tensor.matmul_mx(
                out=bank[:],
                lhsT=codes.bitcast(FP8X4),
                lhsT_scale=scales,
                rhs=picked_words[:].bitcast(FP8X4),
                rhs_scale=picked_scales[4 * z : P, :],
                start=(z == 0),
                stop=(z == PASSES - 1),
            )

        def first_pass(banks, raw, picked_words, picked_scales, name):
            for t0 in range(0, TILES, 1):
                grouped = keep.tile([P, 1 * P * PACK], BF16, name="%s_bf%d" % (name, t0), align_bytes=64)
                for u in range(1):
                    cast(grouped[:, u * P * PACK : (u + 1) * P * PACK], raw, t0 + u, ENG.get((name, t0 + u), "scalar"))
                codes, scales = quantize(grouped, "%s_%d" % (name, t0))
                for u in range(1):
                    cols = slice(u * P, (u + 1) * P)
                    multiply(banks[t0 + u], codes[:, cols], scales[:, cols], picked_words, picked_scales, 0)

        def last_pass(bank, raw, t, picked_words, picked_scales, name):
            grouped = keep.tile([P, P * PACK], BF16, name="%s_bf%d" % (name, t), align_bytes=64)
            cast(grouped[:], raw, t, ENG.get((name, t), "scalar"))
            codes, scales = quantize(grouped, "%s_%d" % (name, t))
            multiply(bank, codes[:], scales[:], picked_words, picked_scales, 1)

        def neg_max(bank, name):
            top = keep.tile([P, 1], F32, name=name)
            nc.vector.tensor_reduce(top[:], bank[:], AXIS_X, ALU.max, negate=True)
            return top

        c_banks = [psum.tile([P, S], F32, name="c_bank%d" % t) for t in range(TILES)]
        y_banks = [psum.tile([P, S], F32, name="y_bank%d" % t) for t in range(TILES)]

        coarse_words0 = gather_words(words0, coarse_list, "coarse_words0")
        fine_words0 = gather_words(words0, offs_list, "fine_words0")
        coarse_scales = gather_scales(coarse_list, "coarse_scales")
        fine_scales = gather_scales(offs_list, "fine_scales")
        first_pass(c_banks, w2_raw0, coarse_words0, coarse_scales, "w2p0")
        coarse_words1 = gather_words(words1, coarse_list, "coarse_words1")
        fine_words1 = gather_words(words1, offs_list, "fine_words1")

        for t in range(TILES):
            last_pass(c_banks[t], w2_raw1, t, coarse_words1, coarse_scales, "w2p1")
        c_top = [neg_max(c_banks[t], "c_top%d" % t) for t in range(TILES)]
        c_sum = keep.tile([P, TILES], F32, name="c_sum")
        y_sum = keep.tile([P, TILES], F32, name="y_sum")
        first_pass(y_banks, w1_raw0, fine_words0, fine_scales, "w1p0")
        for t in range(TILES):
            last_pass(y_banks[t], w1_raw1, t, fine_words1, fine_scales, "w1p1")
        y_top = [neg_max(y_banks[t], "y_top%d" % t) for t in range(TILES)]

        out_rows = out.rearrange("(a t b) j -> t a b j", t=TILES, b=4)
        both = keep.tile([P, TILES], F32, name="both")
        factor = keep.tile([P, TILES], F32, name="factor")
        y_exp = [keep.tile([P, S], F32, name="y_exp%d" % t, align_bytes=64) for t in range(TILES)]
        prod = [keep.tile([P, S], F32, name="prod%d" % t, align_bytes=64) for t in range(TILES)]
        scaled = [keep.tile([P, S], F32, name="scaled%d" % t, align_bytes=64) for t in range(TILES)]

        def exps(t):
            nc.scalar.activation(windows[t][:, :S], c_banks[t][:], ACT.Exp, bias=c_top[t][:], accum_out=c_sum[:, t : t + 1])
            nc.scalar.activation(y_exp[t][:], y_banks[t][:], ACT.Exp, bias=y_top[t][:], accum_out=y_sum[:, t : t + 1])

        def sums(cols):
            nc.vector.scalar_tensor_tensor(both[:, cols], y_sum[:, cols], 1.0 / 512.0, c_sum[:, cols], ALU.mult, ALU.mult)

        def times_parent(t, fine):
            nc.vector.tensor_tensor(prod[t][:], windows[t][:].indirect(par_list[:]), fine[:], ALU.mult)

        def scale(t, vals):
            nc.scalar.activation(scaled[t][:], vals[:], ACT.Copy, scale=factor[:, t : t + 1])

        exps(0)
        times_parent(0, y_exp[0])
        exps(1)
        sums(slice(0, 2))
        nc.vector.reciprocal(factor[:, 0:2], both[:, 0:2])
        times_parent(1, y_exp[1])
        exps(2)
        sums(slice(2, 3))
        nc.vector.reciprocal(factor[:, 2:3], both[:, 2:3])
        exps(3)
        sums(slice(3, 4))
        times_parent(3, y_exp[3])
        nc.vector.reciprocal(factor[:, 3:4], both[:, 3:4])
        scale(0, prod[0])
        nc.sync.dma_start(out_rows[0], scaled[0][:])
        scale(2, y_exp[2])
        times_parent(2, scaled[2])
        scale(1, prod[1])
        nc.sync.dma_start(out_rows[1], scaled[1][:])
        scale(3, prod[3])
        nc.scalar.dma_start(out_rows[3], scaled[3][:])
        nc.sync.dma_start(out_rows[2], prod[2][:])
